import numpy as np, ml_dtypes
CORES = [73,201,329,457,330]
N = 5
F = 128
def setup_inputs(rng):
    x = (rng.standard_normal((N, 128, 128), dtype=np.float32) / 11).astype(ml_dtypes.bfloat16)
    w = rng.standard_normal((128, F), dtype=np.float32).astype(ml_dtypes.bfloat16)
    return {"x": x, "xt": x.transpose(0, 2, 1).copy(), "w": np.broadcast_to(w, (N, 128, F)).copy()}
def setup_inputs_big(rng):
    d = setup_inputs(rng)
    for k in ("x", "xt", "w"): d[k] = (d[k].astype(np.float32) * 1024.0).astype(d[k].dtype)
    return d
def setup_inputs_small(rng):
    d = setup_inputs(rng)
    for k in ("x", "xt", "w"): d[k] = (d[k].astype(np.float32) * (1 / 1024.0)).astype(d[k].dtype)
    return d
def setup_inputs_apart(rng):
    d = setup_inputs(rng)
    f = (10.0 ** rng.permutation(np.linspace(-1.5, 1.5, N))).astype(np.float32).reshape(N, 1, 1)
    for k in ("x", "xt"): d[k] = (d[k].astype(np.float32) * f).astype(d[k].dtype)
    return d
def reference(x, xt, w):
    X, XT, W = x.astype(np.float64), xt.astype(np.float64), w.astype(np.float64)
    s = sum(X[j].T @ (XT[j].T @ W[j]) for j in range(N)).astype(ml_dtypes.bfloat16)
    return {"y": np.broadcast_to(s, (N,) + s.shape)}

from concourse.bass import DstId, RemoteDMATransfer

P = 128
ENGINES = 8
HOP1 = "cable"

SCRATCH = {
    "xs": ("sbuf", [P, P], "bfloat16"),
    "ws": ("sbuf", [P, P], "bfloat16"),
    "lx": ("sbuf", [P, 2 * P], "bfloat16"),
    "lg": ("sbuf", [P, P], "bfloat16"),
    "gb": ("sbuf", [P, P], "bfloat16"),
    "gl": ("sbuf", [P, P], "bfloat16"),
    "yb": ("sbuf", [P, P], "bfloat16"),
    "pa": ("psum", [P, 512], "float32"),
    "pc": ("psum", [P, 512], "float32"),
    "py": ("psum", [P, 512], "float32"),
}
SEMAPHORES = ["ldx", "ldw", "ax0", "ax1", "ag", "sent", "pa", "pc", "py", "da", "dc", "dy", "st"]


def _plan(cores, topo):
    n = len(cores)

    def on_chip(a, b):
        return topo.host(cores[a]) == topo.host(cores[b]) and topo.chip(cores[a]) == topo.chip(cores[b])

    def kind(a, b):
        if topo.same_plane(cores[a], cores[b]):
            return "plane"
        if topo.rack(topo.host(cores[a])) != topo.rack(topo.host(cores[b])) and topo.may_write(cores[a], cores[b]):
            return "cable"
        return None

    lead = [min(j for j in range(n) if on_chip(i, j)) for i in range(n)]
    leaders = [i for i in range(n) if lead[i] == i]
    extras = {a: [i for i in range(n) if lead[i] == a and i != a] for a in leaders}
    one = {a: [b for b in leaders if kind(a, b) == HOP1][0] for a in leaders}
    two = {a: [b for b in leaders if kind(a, b) not in (None, HOP1)][0] for a in leaders}

    xcalls = [[] for _ in range(n)]
    early = [[] for _ in range(n)]
    late = [[] for _ in range(n)]
    fwd = [[] for _ in range(n)]
    for a in leaders:
        xcalls[a].append([one[a]])
        early[one[a]].append(a)
        fwd[a] = [two[a]] + extras[two[a]]
    for t in leaders:
        for e in extras[t]:
            xcalls[e].append([one[t]])
            early[one[t]].append(e)
            xcalls[e].append([t, two[t]])
            late[t].append(e)
            late[two[t]].append(e)
            xcalls[t].append([e])
            early[e].append(t)
            xcalls[one[t]].append([e])
            early[e].append(one[t])
    group = [sorted([i] + early[i]) for i in range(n)]
    for i in range(n):
        got = group[i] + late[i]
        for s in range(n):
            if i in fwd[s]:
                got = got + group[s]
        assert sorted(got) == list(range(n)), (i, got)
        assert len(early[i]) + len(late[i]) <= 2 and len(late[i]) <= 1
    return xcalls, early, late, fwd


def _engines(mask, count):
    out, bit = 0, 1
    while count and bit <= mask:
        if mask & bit:
            out |= bit
            count -= 1
        bit <<= 1
    assert count == 0
    return out


def rank_program(g, core, T, topo):
    me = T.rank_of(core)
    if me is None:
        return
    cores = list(T.cores)
    xcalls, early, late, fwd = _plan(cores, topo)
    S = T.sem
    pe, ve, sy, sc = g.tensor, g.vector, g.sync, g.scalar
    slot_sem = [S.ax0, S.ax1]

    def slot(src, dst):
        return (early[dst] + late[dst]).index(src)

    sent = [0]

    def send(src_ap, dsts, dst_aps, sem):
        mask = topo.mask(core, cores[dsts[0]])
        for d in dsts:
            mask &= topo.mask(core, cores[d])
        mask = _engines(mask, ENGINES)
        ids = []
        for d in dsts:
            rid, pid = topo.addr(cores[d], core)
            ids.append(DstId(rid=rid, pnc=pid))
        if len(dsts) == 1:
            g.remote_dma(out_ap=dst_aps[0], in_ap=src_ap, remote_sem=sem, local_sem=S.sent,
                         pid=ids[0].pnc, routing_id=ids[0].rid, dma_engine_mask=mask)
        else:
            g.remote_dma_fused([RemoteDMATransfer(dst_ids=ids, dma_engine_mask=mask, remote_sem=sem,
                                                  srcs=[src_ap], dsts=dst_aps)], local_sem=S.sent)
        sent[0] += ENGINES

    sy.dma_start(T.xs[:], T.x[:]).then_inc(S.ldx, 16)
    sc.dma_start(T.ws[:], T.w[:]).then_inc(S.ldw, 16)

    g.wait_ge(S.ldx, 16)
    for dsts in xcalls[me]:
        k = slot(me, dsts[0])
        assert all(slot(me, d) == k for d in dsts)
        send(T.xs[:], dsts, [T.lx[:, k * P:(k + 1) * P] for _ in dsts], slot_sem[k])
    if fwd[me]:
        g.wait_ge(S.da, 1)
        send(T.gb[:], fwd[me], [T.lg[:] for _ in fwd[me]], S.ag)
    g.wait_ge(S.sent, sent[0])

    pe.wait_ge(S.ldx, 16)
    mm = pe.matmul(T.pa[:, 0:P], T.xs[:], T.xs[:], True, not early[me])
    for i, s in enumerate(early[me]):
        k = slot(s, me)
        pe.wait_ge(slot_sem[k], ENGINES)
        mm = pe.matmul(T.pa[:, 0:P], T.lx[:, k * P:(k + 1) * P], T.lx[:, k * P:(k + 1) * P], False, i == len(early[me]) - 1)
    mm.then_inc(S.pa, 1)
    for s in late[me]:
        k = slot(s, me)
        pe.wait_ge(slot_sem[k], ENGINES)
        pe.matmul(T.pc[:, 0:P], T.lx[:, k * P:(k + 1) * P], T.lx[:, k * P:(k + 1) * P], True, True).then_inc(S.pc, 1)
    pe.wait_ge(S.ldw, 16)
    pe.wait_ge(S.da, 1)
    pe.matmul(T.py[:, 0:P], T.gb[:], T.ws[:], True, False)
    if late[me]:
        pe.wait_ge(S.dc, 1)
        pe.matmul(T.py[:, 0:P], T.gl[:], T.ws[:], False, False)
    pe.wait_ge(S.ag, ENGINES)
    pe.matmul(T.py[:, 0:P], T.lg[:], T.ws[:], False, True).then_inc(S.py, 1)

    ve.wait_ge(S.pa, 1)
    ve.tensor_copy(T.gb[:], T.pa[:, 0:P]).then_inc(S.da, 1)
    if late[me]:
        ve.wait_ge(S.pc, 1)
        ve.tensor_copy(T.gl[:], T.pc[:, 0:P]).then_inc(S.dc, 1)
    ve.wait_ge(S.py, 1)
    ve.tensor_copy(T.yb[:], T.py[:, 0:P]).then_inc(S.dy, 1)

    sy.wait_ge(S.dy, 1)
    sy.dma_start(T.y[:], T.yb[:]).then_inc(S.st, 16)
    sy.wait_ge(S.st, 16)
